import numpy as np
import ml_dtypes


def mxq(x, axis, fmt="e4m3"):
    dtype, down = {"e4m3": (ml_dtypes.float8_e4m3fn, 7), "e5m2": (ml_dtypes.float8_e5m2, 14)}[fmt]
    v = np.moveaxis(np.asarray(x, np.float32).astype(ml_dtypes.bfloat16).astype(np.float64), axis, -1)
    blocks = v.reshape(v.shape[:-1] + (-1, 32))
    amax = np.abs(blocks).max(-1, keepdims=True)
    byte = np.maximum(np.where(amax > 0, np.frexp(amax)[1] - 1 + 127, 0) - down, 1)
    scale = np.exp2(byte - 127.0)
    codes = (blocks / scale).astype(np.float32).astype(dtype).astype(np.float64)
    return np.moveaxis((codes * scale).reshape(v.shape), -1, axis)


WIDE = False


def mx_kscale(k):
    if not WIDE:
        return np.ones(k)
    levels = np.array([10, -10, 5, -5, 0])
    if k % 512:
        return np.exp2(np.random.permutation(np.resize(levels, k // 32))).repeat(32)
    a = np.empty((k // 512, 16))
    for p in range(k // 512):
        a[p, :8] = np.random.permutation(np.resize(levels, 8))
        for g in range(8):
            far = levels[np.abs(levels - a[p, g]) >= 10]
            a[p, g + 8] = far[np.random.randint(len(far))]
    return np.exp2(a.ravel()).repeat(32)


def f64(x):
    return np.asarray(x).astype(np.float64)


def striped(idx):
    return np.tile(idx.reshape(-1, 16).T, (8, 1)).astype(np.uint16)


def unstriped(offs):
    return offs[:16].T.reshape(-1).astype(np.int64)


E2M1 = np.array([0.0, 0.5, 1.0, 1.5, 2.0, 3.0, 4.0, 6.0, -0.0, -0.5, -1.0, -1.5, -2.0, -3.0, -4.0, -6.0])


def pack_weight(w, fmt):
    k, n = w.shape
    w = f64(np.asarray(w, np.float32).astype(ml_dtypes.bfloat16)).reshape(k // 32, 32, n)
    amax = np.abs(w).max(1)
    if fmt == "e4m3":
        byte = np.frexp(amax)[1] - 1 + 127 - 7
    else:
        mant, ex = np.frexp(amax / 6.0)
        byte = np.where(mant > 0.5, ex, ex - 1) + 127
    byte = np.clip(np.where(amax > 0, byte, 1), 1, 254)
    scaled = (w * np.exp2(127.0 - byte)[:, None, :]).reshape(k, n).astype(np.float32)
    by_word = np.ascontiguousarray(scaled.reshape(k // 512, 128, 4, n).transpose(0, 1, 3, 2))
    if fmt == "e4m3":
        words = by_word.astype(ml_dtypes.float8_e4m3fn).view(np.uint8)
    else:
        c = by_word.astype(ml_dtypes.float4_e2m1fn).view(np.uint8) & 0xF
        words = (c[..., 0::2] | (c[..., 1::2] << 4)).reshape(k // 512, 128, 2 * n)
    return np.ascontiguousarray(words), np.ascontiguousarray(byte.astype(np.uint8).reshape(k // 512, 16, n))


def unpack_weight(words, scales, fmt):
    g, _, n = scales.shape
    words = np.ascontiguousarray(words).reshape(g, 128, n, -1)
    if fmt == "e4m3":
        vals = words.view(ml_dtypes.float8_e4m3fn).astype(np.float64)
    else:
        nib = np.empty((g, 128, n, 4), np.uint8)
        nib[..., 0::2] = words & 0xF
        nib[..., 1::2] = words >> 4
        vals = E2M1[nib]
    vals = vals * np.repeat(np.exp2(scales.astype(np.float64) - 127.0), 8, axis=1)[..., None]
    return vals.transpose(0, 1, 3, 2).reshape(g * 512, n)


def gelu(v):
    return 0.5 * v * (1.0 + np.tanh(np.sqrt(2.0 / np.pi) * (v + 0.044715 * v**3)))


def striped8(idx):
    return np.concatenate([v.reshape(-1, 16).T for v in idx]).astype(np.uint16)


def unstriped8(offs):
    return np.stack([offs[16 * g:16 * g + 16].T.reshape(-1) for g in range(8)]).astype(np.int64)


def heads(h, wgt, idx8):
    r = np.arange(h.shape[0])
    return wgt[r // 4 % 128] * h[r[:, None], idx8[r % 512 // 64]]


K, H, N, T, S, P = 1024, 512, 512, 4096, 1024, 512

def setup_inputs():
    n = np.random.standard_normal
    s = mx_kscale(K)[:, None]
    u = mx_kscale(H)[:, None]
    tab_words, tab_scales = pack_weight(n((K, T)) * s, "e4m3")
    w2_words, w2_scales = pack_weight(n((K, H)) / np.sqrt(K) / s, "e2m1")
    w5_words, w5_scales = pack_weight(n((H, N)) / np.sqrt(H) / u, "e4m3")
    return {
        "tab_words": tab_words, "tab_scales": tab_scales,
        "offs": striped(np.random.permutation(T)[:S]),
        "offs2": striped8(np.stack([np.random.permutation(S)[:P] for _ in range(8)])),
        "offs3": striped8(np.stack([np.random.permutation(S)[:P] for _ in range(8)])),
        "w1": (0.8 * n((K, H)) / np.sqrt(K) / s).astype(np.float32),
        "w2_words": w2_words, "w2_scales": w2_scales,
        "b2": (0.5 * n(H)).astype(np.float32),
        "w3": (0.8 * n((K, H)) / np.sqrt(K) / s).astype(np.float32),
        "wga": np.repeat(np.random.uniform(0.5, 2.0, (8, P)), 16, axis=0).astype(np.float32),
        "wgb": np.repeat(np.random.uniform(0.5, 2.0, (8, P)), 16, axis=0).astype(np.float32),
        "gain": (np.exp(0.3 * n(H)) * u[:, 0]).astype(np.float32),
        "w4": (n((H, N)) / np.sqrt(H) / u).astype(np.float32),
        "w5_words": w5_words, "w5_scales": w5_scales,
        "b5": (0.5 * n(N)).astype(np.float32),
    }

def reference(tab_words, tab_scales, offs, offs2, offs3, w1, w2_words, w2_scales, b2, w3, wga, wgb, gain, w4, w5_words, w5_scales, b5):
    v = unpack_weight(tab_words, tab_scales, "e4m3")[:, unstriped(offs)]
    d1 = mxq(f64(w1), 0, "e4m3").T @ v
    d2 = (unpack_weight(w2_words, w2_scales, "e2m1").T @ v) + f64(b2)[:, None]
    ha = d1 * d2
    hb = mxq(f64(w3), 0, "e4m3").T @ v
    xa = heads(ha, f64(wga), unstriped8(offs2))
    xb = heads(hb, f64(wgb), unstriped8(offs3))
    x = mxq(np.tanh(xa + xb) * f64(gain)[:, None], 0, "e4m3")
    y4 = mxq(f64(w4), 0, "e4m3").T @ x
    y5 = (unpack_weight(w5_words, w5_scales, "e4m3").T @ x) + f64(b5)[:, None]
    return np.maximum(y4, y5)

@@ -1,0 +1,233 @@
+from contextlib import ExitStack
+
+import concourse.mybir as mybir
+
+K, H, N, T, S, M = 1024, 512, 512, 4096, 1024, 512
+FLOPS = 2 * (3 * K * H * S + 2 * H * N * M)
+
+F32 = mybir.dt.float32
+BF16 = mybir.dt.bfloat16
+I32 = mybir.dt.int32
+U32 = mybir.dt.uint32
+U16 = mybir.dt.uint16
+U8 = mybir.dt.uint8
+FP8X4 = mybir.dt.float8_e4m3fn_x4
+FP4X4 = mybir.dt.float4_e2m1fn_x4
+ALU = mybir.AluOpType
+ACT = mybir.ActivationFunctionType
+
+P = 128
+PACK = 4
+PASSES = K // (P * PACK)
+BANK = 512
+HALVES = S // BANK
+M_PART = 256
+
+
+def tile_list_calf_block_scores_kernel(
+    tc, tab_words, tab_scales, offs, offs2, offs3, w1, w2_words, w2_scales, b2, w3, wga, wgb, gain, w4, w5_words, w5_scales, b5, out
+):
+    nc = tc.nc
+    with ExitStack() as ctx:
+        keep = ctx.enter_context(tc.tile_pool(name="keep", bufs=1))
+        work = ctx.enter_context(tc.tile_pool(name="work", bufs=4))
+        psum = ctx.enter_context(tc.psum_pool(name="psum", bufs=8))
+
+        def held(shape, dtype, name):
+            return keep.tile(shape, dtype, name=name, align_bytes=64)
+
+        scale_window = held([P, T // 4], I32, "scale_window")
+        nc.vector.memset(scale_window[:], 0)
+        w2_scales_raw = held([P, PASSES * H // 4], I32, "w2_scales_raw")
+        nc.vector.memset(w2_scales_raw[:], 0)
+        v_planes = [held([P, S // 4], I32, "v_plane%d" % a) for a in range(PASSES)]
+        for a in range(PASSES):
+            nc.vector.memset(v_planes[a][:], 0)
+        w5_plane = held([P, N // 4], I32, "w5_plane")
+        nc.vector.memset(w5_plane[:], 0)
+
+        idx = keep.tile([P, S // 16], U16, name="idx")
+        nc.sync.dma_start(idx[:], offs)
+        tab = [held([P, T], I32, "tab%d" % a) for a in range(PASSES)]
+        nc.sync.dma_start(tab[0][:], tab_words[0].rearrange("p t i -> p (t i)").bitcast(I32))
+        nc.scalar.dma_start(scale_window[0:P:4, :], tab_scales.rearrange("a q t -> (a q) t").bitcast(I32))
+        w2_raw = held([P, PASSES * H // 2], I32, "w2_raw")
+        nc.scalar.dma_start(
+            w2_raw[:].rearrange("p (a c) -> p a c", a=PASSES), w2_words.rearrange("a p c -> p a c").bitcast(I32)
+        )
+        nc.sync.dma_start(tab[1][:], tab_words[1].rearrange("p t i -> p (t i)").bitcast(I32))
+        for q in range(4):
+            nc.scalar.dma_start(
+                w2_scales_raw[32 * q : 32 * q + 4, :].rearrange("r (a c) -> r a c", a=PASSES),
+                w2_scales[:, 4 * q : 4 * q + 4, :].rearrange("a r c -> r a c").bitcast(I32),
+            )
+        b2_sb = held([P, PACK], F32, "b2_sb")
+        nc.scalar.dma_start(b2_sb[:], b2.rearrange("(p t) -> p t", t=PACK))
+
+        def load_rows(w, a, name):
+            raw = held([P, PACK, H], F32, name)
+            nc.sync.dma_start(raw[:], w[512 * a : 512 * (a + 1), :].rearrange("(p j) c -> p j c", j=PACK))
+            return raw
+
+        w1_raw = [load_rows(w1, a, "w1_raw%d" % a) for a in range(PASSES)]
+        idx_a = keep.tile([P, M // 16], U16, name="idx_a")
+        nc.sync.dma_start(idx_a[:], offs2)
+        wga_sb = held([P, M], F32, "wga_sb")
+        nc.sync.dma_start(wga_sb[:], wga)
+        w3_raw = [load_rows(w3, a, "w3_raw%d" % a) for a in range(PASSES)]
+        idx_b = keep.tile([P, M // 16], U16, name="idx_b")
+        nc.sync.dma_start(idx_b[:], offs3)
+        wgb_sb = held([P, M], F32, "wgb_sb")
+        nc.sync.dma_start(wgb_sb[:], wgb)
+        gain_sb = held([P, PACK], F32, "gain_sb")
+        nc.sync.dma_start(gain_sb[:], gain.rearrange("(p t) -> p t", t=PACK))
+        w4_raw = load_rows(w4, 0, "w4_raw")
+        w5_codes = held([P, N], I32, "w5_codes")
+        nc.sync.dma_start(w5_codes[:], w5_words[0].rearrange("p c i -> p (c i)").bitcast(I32))
+        for q in range(4):
+            nc.sync.dma_start(w5_plane[32 * q : 32 * q + 4, :], w5_scales[0, 4 * q : 4 * q + 4, :].bitcast(I32))
+        b5_sb = held([P, N // P], F32, "b5_sb")
+        with nc.allow_non_contiguous_dma(reason="one bias value a partition"):
+            nc.sync.dma_start(b5_sb[:], b5.rearrange("(c p) -> p c", p=P))
+
+        picked_scales = held([P, S], U8, "picked_scales")
+        nc.vector.tensor_copy(picked_scales[:], scale_window[:].bitcast(U8).indirect(idx[:]))
+        for a in range(PASSES):
+            for q in range(4):
+                first = 4 * (16 * a + 4 * q)
+                nc.scalar.dma_start(v_planes[a][32 * q : 32 * q + 4, :], picked_scales[first : first + 13 : 4, :].bitcast(I32))
+
+        w2_codes = held([P, PASSES * H * 2], U8, "w2_codes")
+        w2_plane = held([P, PASSES * H], U8, "w2_plane")
+        for a in range(PASSES):
+            nc.vector.tensor_copy(
+                w2_codes[:, 2 * H * a : 2 * H * (a + 1)].rearrange("p (t m e) -> p m t e", t=PACK, e=2),
+                w2_raw[:].bitcast(U8)[:, 2 * H * a : 2 * H * (a + 1)].rearrange("p (m t e) -> p m t e", t=PACK, e=2),
+            )
+        nc.vector.tensor_copy(
+            w2_plane[:].rearrange("p (a t m) -> p a m t", a=PASSES, t=PACK),
+            w2_scales_raw[:].bitcast(U8).rearrange("p (a m t) -> p a m t", a=PASSES, t=PACK),
+        )
+
+        v_codes = [[held([P, BANK], U32, "v_codes%d_%d" % (a, h)) for h in range(HALVES)] for a in range(PASSES)]
+        for a in range(PASSES):
+            for h in range(HALVES):
+                nc.vector.tensor_copy(v_codes[a][h][:], tab[a][:].bitcast(U32).indirect(idx[:, 32 * h : 32 * (h + 1)]))
+
+        def first_stage(codes_of, plane_of, fmt, t, h):
+            acc = psum.tile([P, BANK], F32, name="acc", tag="acc")
+            for a in range(PASSES):
+                nc.tensor.matmul_mx(
+                    out=acc[:],
+                    lhsT=codes_of(a, t).bitcast(fmt),
+                    lhsT_scale=plane_of(a, t),
+                    rhs=v_codes[a][h][:].bitcast(FP8X4),
+                    rhs_scale=v_planes[a][:].bitcast(U8)[:, BANK * h : BANK * (h + 1)],
+                    start=(a == 0),
+                    stop=(a == PASSES - 1),
+                )
+            return acc
+
+        d2b = [held([P, S], F32, "d2b%d" % t) for t in range(PACK)]
+        for t in range(PACK):
+            for h in range(HALVES):
+                acc = first_stage(
+                    lambda a, t: w2_codes[:, 2 * (H * a + P * t) : 2 * (H * a + P * (t + 1))],
+                    lambda a, t: w2_plane[:, H * a + P * t : H * a + P * (t + 1)],
+                    FP4X4, t, h,
+                )
+                nc.scalar.activation(d2b[t][:, BANK * h : BANK * (h + 1)], acc[:], ACT.Identity, bias=b2_sb[:, t : t + 1])
+
+        def round_dealt(copy, raw, name):
+            grouped = held([P, PACK * H], BF16, name)
+            copy(
+                grouped[:].rearrange("p (t m j) -> p m j t", t=PACK, j=PACK),
+                raw[:].rearrange("p j (m t) -> p m j t", t=PACK),
+            )
+            return grouped
+
+        def quantize(grouped, name, pieces):
+            width = grouped.shape[1] // PACK
+            codes = held([P, width], U32, name + "_codes")
+            plane = held([P, width], U8, name + "_plane")
+            step = width // pieces
+            for c in range(0, width, step):
+                nc.vector.quantize_mx(
+                    out=codes[:, c : c + step].bitcast(FP8X4),
+                    scales=plane[:, c : c + step],
+                    in_=grouped[:, PACK * c : PACK * (c + step)],
+                )
+            return codes, plane
+
+        w1_q = [quantize(round_dealt(nc.vector.tensor_copy, w1_raw[a], "w1_bf%d" % a), "w1_%d" % a, 1 + a) for a in range(PASSES)]
+        w3_bf = [round_dealt(nc.scalar.copy, w3_raw[a], "w3_bf%d" % a) for a in range(PASSES)]
+
+        def stage_of(q, t, h):
+            return first_stage(
+                lambda a, t: q[a][0][:, P * t : P * (t + 1)], lambda a, t: q[a][1][:, P * t : P * (t + 1)], FP8X4, t, h
+            )
+
+        xa = [held([P, M], F32, "xa%d" % t) for t in range(PACK)]
+        for t in range(PACK):
+            ha = held([P, S], F32, "ha%d" % t)
+            for h in range(HALVES):
+                acc = stage_of(w1_q, t, h)
+                cols = slice(BANK * h, BANK * (h + 1))
+                nc.vector.tensor_tensor(ha[:, cols], acc[:], d2b[t][:, cols], ALU.mult)
+            nc.vector.tensor_tensor(xa[t][:], ha[:].indirect(idx_a[:]), wga_sb[:], ALU.mult)
+
+        w3_q = [quantize(w3_bf[a], "w3_%d" % a, 1) for a in range(PASSES)]
+        hb = [held([P, S], F32, "hb%d" % t) for t in range(PACK)]
+        for t in range(PACK):
+            for h in range(HALVES):
+                acc = stage_of(w3_q, t, h)
+                nc.scalar.copy(hb[t][:, BANK * h : BANK * (h + 1)], acc[:])
+
+        w4_bf = held([P, PACK * N], BF16, "w4_bf")
+        nc.scalar.copy(
+            w4_bf[:].rearrange("p (c i j) -> p c j i", i=4, j=PACK), w4_raw[:].rearrange("p j (c i) -> p c j i", i=4)
+        )
+        w4_codes, w4_plane = quantize(w4_bf, "w4", 1)
+
+        for part in range(M // M_PART):
+            cols = slice(M_PART * part, M_PART * (part + 1))
+            x_rows = held([P, PACK, M_PART], BF16, "x_rows%d" % part)
+            for t in range(PACK):
+                xb = work.tile([P, M_PART], F32, name="xb")
+                nc.vector.tensor_tensor(
+                    xb[:], hb[t][:].indirect(idx_b[:, M_PART // 16 * part : M_PART // 16 * (part + 1)]), wgb_sb[:, cols], ALU.mult
+                )
+                z = work.tile([P, M_PART], F32, name="z")
+                nc.vector.tensor_tensor(z[:], xa[t][:, cols], xb[:], ALU.add)
+                bent = work.tile([P, M_PART], F32, name="bent")
+                nc.scalar.activation(bent[:], z[:], ACT.Tanh)
+                nc.scalar.activation(x_rows[:, t, :], bent[:], ACT.Copy, scale=gain_sb[:, t : t + 1])
+            x_bf = held([P, PACK * M_PART], BF16, "x_bf%d" % part)
+            nc.vector.tensor_copy(
+                x_bf[:].rearrange("p (c i t) -> p c t i", i=4, t=PACK), x_rows[:].rearrange("p t (c i) -> p c t i", i=4)
+            )
+            x_codes, x_plane = quantize(x_bf, "x%d" % part, 1)
+            for pair in range(N // P // 2):
+                y4 = psum.tile([P, 2, M_PART], F32, name="y4", tag="acc")
+                y5 = psum.tile([P, 2, M_PART], F32, name="y5", tag="acc")
+                y5b = held([P, 2, M_PART], F32, "y5b%d_%d" % (part, pair))
+                for i in range(2):
+                    n_cols = slice(P * (2 * pair + i), P * (2 * pair + i + 1))
+                    nc.tensor.matmul_mx(
+                        out=y5[:, i, :], lhsT=w5_codes[:, n_cols].bitcast(FP8X4), lhsT_scale=w5_plane[:].bitcast(U8)[:, n_cols],
+                        rhs=x_codes[:].bitcast(FP8X4), rhs_scale=x_plane[:], start=True, stop=True,
+                    )
+                for i in range(2):
+                    n_cols = slice(P * (2 * pair + i), P * (2 * pair + i + 1))
+                    nc.tensor.matmul_mx(
+                        out=y4[:, i, :], lhsT=w4_codes[:, n_cols].bitcast(FP8X4), lhsT_scale=w4_plane[:, n_cols],
+                        rhs=x_codes[:].bitcast(FP8X4), rhs_scale=x_plane[:], start=True, stop=True,
+                    )
+                for i in range(2):
+                    c = 2 * pair + i
+                    nc.scalar.activation(y5b[:, i, :], y5[:, i, :], ACT.Identity, bias=b5_sb[:, c : c + 1])
+                best = held([P, 2, M_PART], F32, "best%d_%d" % (part, pair))
+                nc.vector.tensor_tensor(best[:], y4[:], y5b[:], ALU.max)
+                nc.sync.dma_start(
+                    out[2 * P * pair : 2 * P * (pair + 1), cols].rearrange("(i p) m -> p i m", p=P), best[:]
+                )

@@ -30,89 +30,103 @@ def tile_list_calf_block_scores_kernel(
     nc = tc.nc
     with ExitStack() as ctx:
         keep = ctx.enter_context(tc.tile_pool(name="keep", bufs=1))
+        stream = ctx.enter_context(tc.tile_pool(name="stream", bufs=1))
         work = ctx.enter_context(tc.tile_pool(name="work", bufs=4))
         psum = ctx.enter_context(tc.psum_pool(name="psum", bufs=8))
 
-        def held(shape, dtype, name):
-            return keep.tile(shape, dtype, name=name, align_bytes=64)
+        def held(shape, dtype, name, after=None):
+            return keep.tile(shape, dtype, name=name, tag=after or name, align_bytes=64)
 
-        scale_window = held([P, T // 4], I32, "scale_window")
-        nc.vector.memset(scale_window[:], 0)
+        def placed(shape, dtype, name, kib):
+            return stream.tile(shape, dtype, name=name, align_bytes=64, offset=int(1024 * kib))
+
+        scale_windows = held([P, PASSES * T // 4], I32, "scale_windows")
+        nc.vector.memset(scale_windows[:], 0)
+
         w2_scales_raw = held([P, PASSES * H // 4], I32, "w2_scales_raw")
-        nc.vector.memset(w2_scales_raw[:], 0)
-        v_planes = [held([P, S // 4], I32, "v_plane%d" % a) for a in range(PASSES)]
-        for a in range(PASSES):
-            nc.vector.memset(v_planes[a][:], 0)
-        w5_plane = held([P, N // 4], I32, "w5_plane")
-        nc.vector.memset(w5_plane[:], 0)
+        nc.gpsimd.memset(w2_scales_raw[:], 0)
 
         idx = keep.tile([P, S // 16], U16, name="idx")
         nc.sync.dma_start(idx[:], offs)
-        tab = [held([P, T], I32, "tab%d" % a) for a in range(PASSES)]
-        nc.sync.dma_start(tab[0][:], tab_words[0].rearrange("p t i -> p (t i)").bitcast(I32))
-        nc.scalar.dma_start(scale_window[0:P:4, :], tab_scales.rearrange("a q t -> (a q) t").bitcast(I32))
-        w2_raw = held([P, PASSES * H // 2], I32, "w2_raw")
-        nc.scalar.dma_start(
+        w2_raw = placed([P, PASSES * H // 2], I32, "w2_raw", 19)
+        nc.sync.dma_start(
             w2_raw[:].rearrange("p (a c) -> p a c", a=PASSES), w2_words.rearrange("a p c -> p a c").bitcast(I32)
         )
-        nc.sync.dma_start(tab[1][:], tab_words[1].rearrange("p t i -> p (t i)").bitcast(I32))
+        idx_a = keep.tile([P, M // 16], U16, name="idx_a")
+        nc.sync.dma_start(idx_a[:], offs2)
+        idx_b = keep.tile([P, M // 16], U16, name="idx_b")
+        nc.sync.dma_start(idx_b[:], offs3)
+
+        def load_table(a, kib):
+            words = placed([P, T], I32, "tab%d" % a, kib)
+            nc.sync.dma_start(words[:], tab_words[a].rearrange("p t i -> p (t i)").bitcast(I32))
+            return words
+
+        def load_rows(w, a, raw):
+            nc.sync.dma_start(raw[:], w[512 * a : 512 * (a + 1), :].rearrange("(p j) c -> p j c", j=PACK))
+            return raw
+
+        tab = [load_table(0, 0)]
+        w1_raw = [load_rows(w1, 0, held([P, PACK, H], F32, "w1_raw0"))]
         for q in range(4):
             nc.scalar.dma_start(
+                scale_windows[32 * q : 32 * q + 4, :].rearrange("r (a c) -> r a c", a=PASSES),
+                tab_scales[:, 4 * q : 4 * q + 4, :].rearrange("a r c -> r a c").bitcast(I32),
+            )
+        for q in range(4):
+            nc.gpsimd.dma_start(
                 w2_scales_raw[32 * q : 32 * q + 4, :].rearrange("r (a c) -> r a c", a=PASSES),
                 w2_scales[:, 4 * q : 4 * q + 4, :].rearrange("a r c -> r a c").bitcast(I32),
             )
         b2_sb = held([P, PACK], F32, "b2_sb")
-        nc.scalar.dma_start(b2_sb[:], b2.rearrange("(p t) -> p t", t=PACK))
+        nc.gpsimd.dma_start(b2_sb[:], b2.rearrange("(p t) -> p t", t=PACK))
 
-        def load_rows(w, a, name):
-            raw = held([P, PACK, H], F32, name)
-            nc.sync.dma_start(raw[:], w[512 * a : 512 * (a + 1), :].rearrange("(p j) c -> p j c", j=PACK))
-            return raw
+        w2_codes = held([P, PASSES * H], U16, "w2_codes")
+        nc.vector.tensor_copy(
+            w2_codes[:].rearrange("p (a t m) -> p a m t", a=PASSES, t=PACK),
+            w2_raw[:].bitcast(U16).rearrange("p (a m t) -> p a m t", a=PASSES, t=PACK),
+        )
+        tab.append(load_table(1, 19))
 
-        w1_raw = [load_rows(w1, a, "w1_raw%d" % a) for a in range(PASSES)]
-        idx_a = keep.tile([P, M // 16], U16, name="idx_a")
-        nc.sync.dma_start(idx_a[:], offs2)
-        wga_sb = held([P, M], F32, "wga_sb")
+        v_planes = [held([P, S], U8, "v_plane%d" % a) for a in range(PASSES)]
+        for a in range(PASSES):
+            nc.vector.tensor_copy(v_planes[a][:], scale_windows[:].bitcast(U8)[:, T * a : T * (a + 1)].indirect(idx[:]))
+        v_codes = [
+            [held([P, BANK], U32, "v_codes%d_%d" % (a, h), "scale_windows" if a + h == 0 else None) for h in range(HALVES)]
+            for a in range(PASSES)
+        ]
+
+        def gather_words(a):
+            for h in range(HALVES):
+                nc.vector.tensor_copy(v_codes[a][h][:], tab[a][:].bitcast(U32).indirect(idx[:, 32 * h : 32 * (h + 1)]))
+
+        gather_words(0)
+        w1_raw.append(load_rows(w1, 1, placed([P, PACK, H], F32, "w1_raw1", 0)))
+        wga_sb = placed([P, M], F32, "wga_sb", 8)
         nc.sync.dma_start(wga_sb[:], wga)
-        w3_raw = [load_rows(w3, a, "w3_raw%d" % a) for a in range(PASSES)]
-        idx_b = keep.tile([P, M // 16], U16, name="idx_b")
-        nc.sync.dma_start(idx_b[:], offs3)
-        wgb_sb = held([P, M], F32, "wgb_sb")
-        nc.sync.dma_start(wgb_sb[:], wgb)
-        gain_sb = held([P, PACK], F32, "gain_sb")
-        nc.sync.dma_start(gain_sb[:], gain.rearrange("(p t) -> p t", t=PACK))
-        w4_raw = load_rows(w4, 0, "w4_raw")
-        w5_codes = held([P, N], I32, "w5_codes")
-        nc.sync.dma_start(w5_codes[:], w5_words[0].rearrange("p c i -> p (c i)").bitcast(I32))
-        for q in range(4):
-            nc.sync.dma_start(w5_plane[32 * q : 32 * q + 4, :], w5_scales[0, 4 * q : 4 * q + 4, :].bitcast(I32))
-        b5_sb = held([P, N // P], F32, "b5_sb")
-        with nc.allow_non_contiguous_dma(reason="one bias value a partition"):
-            nc.sync.dma_start(b5_sb[:], b5.rearrange("(c p) -> p c", p=P))
-
-        picked_scales = held([P, S], U8, "picked_scales")
-        nc.vector.tensor_copy(picked_scales[:], scale_window[:].bitcast(U8).indirect(idx[:]))
-        for a in range(PASSES):
-            for q in range(4):
-                first = 4 * (16 * a + 4 * q)
-                nc.scalar.dma_start(v_planes[a][32 * q : 32 * q + 4, :], picked_scales[first : first + 13 : 4, :].bitcast(I32))
-
-        w2_codes = held([P, PASSES * H * 2], U8, "w2_codes")
-        w2_plane = held([P, PASSES * H], U8, "w2_plane")
-        for a in range(PASSES):
-            nc.vector.tensor_copy(
-                w2_codes[:, 2 * H * a : 2 * H * (a + 1)].rearrange("p (t m e) -> p m t e", t=PACK, e=2),
-                w2_raw[:].bitcast(U8)[:, 2 * H * a : 2 * H * (a + 1)].rearrange("p (m t e) -> p m t e", t=PACK, e=2),
-            )
+        w3_raw = [load_rows(w3, 0, placed([P, PACK, H], F32, "w3_raw0", 11))]
+        w2_plane = placed([P, PASSES * H], U8, "w2_plane", 10)
         nc.vector.tensor_copy(
             w2_plane[:].rearrange("p (a t m) -> p a m t", a=PASSES, t=PACK),
             w2_scales_raw[:].bitcast(U8).rearrange("p (a m t) -> p a m t", a=PASSES, t=PACK),
         )
 
-        v_codes = [[held([P, BANK], U32, "v_codes%d_%d" % (a, h)) for h in range(HALVES)] for a in range(PASSES)]
-        for a in range(PASSES):
-            for h in range(HALVES):
-                nc.vector.tensor_copy(v_codes[a][h][:], tab[a][:].bitcast(U32).indirect(idx[:, 32 * h : 32 * (h + 1)]))
+        gather_words(1)
+        w3_raw.append(load_rows(w3, 1, placed([P, PACK, H], F32, "w3_raw1", 19)))
+        wgb_sb = placed([P, M], F32, "wgb_sb", 27)
+        nc.sync.dma_start(wgb_sb[:], wgb)
+        gain_sb = placed([P, PACK], F32, "gain_sb", 31)
+        nc.sync.dma_start(gain_sb[:], gain.rearrange("(p t) -> p t", t=PACK))
+        w4_raw = load_rows(w4, 0, placed([P, PACK, H], F32, "w4_raw", 32))
+        w5_codes = placed([P, N], I32, "w5_codes", 29)
+        nc.sync.dma_start(w5_codes[:], w5_words[0].rearrange("p c i -> p (c i)").bitcast(I32))
+        w5_plane = placed([P, N // 4], I32, "w5_plane", 31.25)
+        nc.gpsimd.memset(w5_plane[:], 0)
+        for q in range(4):
+            nc.sync.dma_start(w5_plane[32 * q : 32 * q + 4, :], w5_scales[0, 4 * q : 4 * q + 4, :].bitcast(I32))
+        b5_sb = placed([P, N // P], F32, "b5_sb", 31.125)
+        with nc.allow_non_contiguous_dma(reason="one bias value a partition"):
+            nc.sync.dma_start(b5_sb[:], b5.rearrange("(c p) -> p c", p=P))
 
         def first_stage(codes_of, plane_of, fmt, t, h):
             acc = psum.tile([P, BANK], F32, name="acc", tag="acc")
@@ -122,21 +136,11 @@ def tile_list_calf_block_scores_kernel(
                     lhsT=codes_of(a, t).bitcast(fmt),
                     lhsT_scale=plane_of(a, t),
                     rhs=v_codes[a][h][:].bitcast(FP8X4),
-                    rhs_scale=v_planes[a][:].bitcast(U8)[:, BANK * h : BANK * (h + 1)],
+                    rhs_scale=v_planes[a][:, BANK * h : BANK * (h + 1)],
                     start=(a == 0),
                     stop=(a == PASSES - 1),
                 )
             return acc
-
-        d2b = [held([P, S], F32, "d2b%d" % t) for t in range(PACK)]
-        for t in range(PACK):
-            for h in range(HALVES):
-                acc = first_stage(
-                    lambda a, t: w2_codes[:, 2 * (H * a + P * t) : 2 * (H * a + P * (t + 1))],
-                    lambda a, t: w2_plane[:, H * a + P * t : H * a + P * (t + 1)],
-                    FP4X4, t, h,
-                )
-                nc.scalar.activation(d2b[t][:, BANK * h : BANK * (h + 1)], acc[:], ACT.Identity, bias=b2_sb[:, t : t + 1])
 
         def round_dealt(copy, raw, name):
             grouped = held([P, PACK * H], BF16, name)
@@ -159,8 +163,20 @@ def tile_list_calf_block_scores_kernel(
                 )
             return codes, plane
 
-        w1_q = [quantize(round_dealt(nc.vector.tensor_copy, w1_raw[a], "w1_bf%d" % a), "w1_%d" % a, 1 + a) for a in range(PASSES)]
-        w3_bf = [round_dealt(nc.scalar.copy, w3_raw[a], "w3_bf%d" % a) for a in range(PASSES)]
+        w1_q = [quantize(round_dealt(nc.scalar.copy, w1_raw[0], "w1_bf0"), "w1_0", 1)]
+
+        d2b = [held([P, S], F32, "d2b%d" % t) for t in range(PACK)]
+        for t in range(PACK):
+            for h in range(HALVES):
+                acc = first_stage(
+                    lambda a, t: w2_codes[:, H * a + P * t : H * a + P * (t + 1)],
+                    lambda a, t: w2_plane[:, H * a + P * t : H * a + P * (t + 1)],
+                    FP4X4, t, h,
+                )
+                nc.scalar.activation(d2b[t][:, BANK * h : BANK * (h + 1)], acc[:], ACT.Identity, bias=b2_sb[:, t : t + 1])
+
+        w1_q.append(quantize(round_dealt(nc.vector.tensor_copy, w1_raw[1], "w1_bf1"), "w1_1", 2))
+        w3_q = [quantize(round_dealt(nc.scalar.copy, w3_raw[a], "w3_bf%d" % a), "w3_%d" % a, 1) for a in range(PASSES)]
 
         def stage_of(q, t, h):
             return first_stage(
@@ -169,14 +185,13 @@ def tile_list_calf_block_scores_kernel(
 
         xa = [held([P, M], F32, "xa%d" % t) for t in range(PACK)]
         for t in range(PACK):
-            ha = held([P, S], F32, "ha%d" % t)
+            ha = held([P, S], F32, "ha%d" % t, after="w3_bf1" if t == PACK - 1 else None)
             for h in range(HALVES):
                 acc = stage_of(w1_q, t, h)
                 cols = slice(BANK * h, BANK * (h + 1))
                 nc.vector.tensor_tensor(ha[:, cols], acc[:], d2b[t][:, cols], ALU.mult)
             nc.vector.tensor_tensor(xa[t][:], ha[:].indirect(idx_a[:]), wga_sb[:], ALU.mult)
 
-        w3_q = [quantize(w3_bf[a], "w3_%d" % a, 1) for a in range(PASSES)]
         hb = [held([P, S], F32, "hb%d" % t) for t in range(PACK)]
         for t in range(PACK):
             for h in range(HALVES):
@@ -184,9 +199,11 @@ def tile_list_calf_block_scores_kernel(
                 nc.scalar.copy(hb[t][:, BANK * h : BANK * (h + 1)], acc[:])
 
         w4_bf = held([P, PACK * N], BF16, "w4_bf")
-        nc.scalar.copy(
-            w4_bf[:].rearrange("p (c i j) -> p c j i", i=4, j=PACK), w4_raw[:].rearrange("p j (c i) -> p c j i", i=4)
-        )
+        for c in range(0, N, P):
+            nc.scalar.copy(
+                w4_bf[:, PACK * c : PACK * (c + P)].rearrange("p (c i j) -> p c j i", i=4, j=PACK),
+                w4_raw[:, :, c : c + P].rearrange("p j (c i) -> p c j i", i=4),
+            )
         w4_codes, w4_plane = quantize(w4_bf, "w4", 1)
 
         for part in range(M // M_PART):

@@ -21,7 +21,7 @@ PACK = 4
 PASSES = K // (P * PACK)
 BANK = 512
 HALVES = S // BANK
-M_PART = 256
+M_PARTS = (slice(0, 256), slice(256, 384), slice(384, 512))
 
 
 def tile_list_calf_block_scores_kernel(
@@ -32,7 +32,7 @@ def tile_list_calf_block_scores_kernel(
         keep = ctx.enter_context(tc.tile_pool(name="keep", bufs=1))
         stream = ctx.enter_context(tc.tile_pool(name="stream", bufs=1))
         work = ctx.enter_context(tc.tile_pool(name="work", bufs=4))
-        psum = ctx.enter_context(tc.psum_pool(name="psum", bufs=8))
+        psum = ctx.enter_context(tc.psum_pool(name="psum", bufs=4))
 
         def held(shape, dtype, name, after=None):
             return keep.tile(shape, dtype, name=name, tag=after or name, align_bytes=64)
@@ -40,15 +40,20 @@ def tile_list_calf_block_scores_kernel(
         def placed(shape, dtype, name, kib):
             return stream.tile(shape, dtype, name=name, align_bytes=64, offset=int(1024 * kib))
 
-        scale_windows = held([P, PASSES * T // 4], I32, "scale_windows")
-        nc.vector.memset(scale_windows[:], 0)
-
-        w2_scales_raw = held([P, PASSES * H // 4], I32, "w2_scales_raw")
-        nc.gpsimd.memset(w2_scales_raw[:], 0)
+        rows = PASSES * 16
+        scale_window = held([P, T // 4], I32, "scale_window")
+        w2_scales_raw = held([P, H // 4], I32, "w2_scales_raw")
+        for tile in (scale_window, w2_scales_raw):
+            nc.vector.memset(tile[rows:64, :], 0)
+            nc.vector.memset(tile[64:P, :], 0)
+        planes = held([P, PASSES * (S + H) // 4], I32, "planes")
+        nc.vector.memset(planes[:], 0)
 
         idx = keep.tile([P, S // 16], U16, name="idx")
         nc.sync.dma_start(idx[:], offs)
-        w2_raw = placed([P, PASSES * H // 2], I32, "w2_raw", 19)
+        nc.sync.dma_start(scale_window[0:rows, :], tab_scales.rearrange("a q t -> (a q) t").bitcast(I32))
+        nc.sync.dma_start(w2_scales_raw[0:rows, :], w2_scales.rearrange("a q c -> (a q) c").bitcast(I32))
+        w2_raw = held([P, PASSES * H // 2], I32, "w2_raw")
         nc.sync.dma_start(
             w2_raw[:].rearrange("p (a c) -> p a c", a=PASSES), w2_words.rearrange("a p c -> p a c").bitcast(I32)
         )
@@ -56,6 +61,8 @@ def tile_list_calf_block_scores_kernel(
         nc.sync.dma_start(idx_a[:], offs2)
         idx_b = keep.tile([P, M // 16], U16, name="idx_b")
         nc.sync.dma_start(idx_b[:], offs3)
+        b2_sb = held([P, PACK], F32, "b2_sb")
+        nc.sync.dma_start(b2_sb[:], b2.rearrange("(p t) -> p t", t=PACK))
 
         def load_table(a, kib):
             words = placed([P, T], I32, "tab%d" % a, kib)
@@ -67,34 +74,37 @@ def tile_list_calf_block_scores_kernel(
             return raw
 
         tab = [load_table(0, 0)]
-        w1_raw = [load_rows(w1, 0, held([P, PACK, H], F32, "w1_raw0"))]
-        for q in range(4):
-            nc.scalar.dma_start(
-                scale_windows[32 * q : 32 * q + 4, :].rearrange("r (a c) -> r a c", a=PASSES),
-                tab_scales[:, 4 * q : 4 * q + 4, :].rearrange("a r c -> r a c").bitcast(I32),
+        w1_raw = [load_rows(w1, 0, placed([P, PACK, H], F32, "w1_raw0", 35))]
+
+        picked_scales = placed([P, S], U8, "picked_scales", 19)
+        nc.vector.tensor_copy(picked_scales[:], scale_window[:].bitcast(U8).indirect(idx[:]))
+        scale_rows = held([P, S + H], U8, "scale_rows")
+        nc.vector.tensor_copy(
+            scale_rows[:, S:].rearrange("p (t m) -> p m t", t=PACK),
+            w2_scales_raw[:].bitcast(U8).rearrange("p (m t) -> p m t", t=PACK),
+        )
+        nc.vector.tensor_copy(scale_rows[:, :S].bitcast(I32), picked_scales[:].bitcast(I32))
+
+        def place_scale_rows(a, q):
+            width = (S + H) // 4
+            first = 16 * a + 4 * q
+            nc.sync.dma_start(
+                planes[32 * q : 32 * q + 4, width * a : width * (a + 1)], scale_rows[first : first + 4, :].bitcast(I32)
             )
+
         for q in range(4):
-            nc.gpsimd.dma_start(
-                w2_scales_raw[32 * q : 32 * q + 4, :].rearrange("r (a c) -> r a c", a=PASSES),
-                w2_scales[:, 4 * q : 4 * q + 4, :].rearrange("a r c -> r a c").bitcast(I32),
-            )
-        b2_sb = held([P, PACK], F32, "b2_sb")
-        nc.gpsimd.dma_start(b2_sb[:], b2.rearrange("(p t) -> p t", t=PACK))
+            place_scale_rows(0, q)
+        tab.append(load_table(1, 19))
+        for q in range(4):
+            place_scale_rows(1, q)
 
         w2_codes = held([P, PASSES * H], U16, "w2_codes")
         nc.vector.tensor_copy(
             w2_codes[:].rearrange("p (a t m) -> p a m t", a=PASSES, t=PACK),
             w2_raw[:].bitcast(U16).rearrange("p (a m t) -> p a m t", a=PASSES, t=PACK),
         )
-        tab.append(load_table(1, 19))
 
-        v_planes = [held([P, S], U8, "v_plane%d" % a) for a in range(PASSES)]
-        for a in range(PASSES):
-            nc.vector.tensor_copy(v_planes[a][:], scale_windows[:].bitcast(U8)[:, T * a : T * (a + 1)].indirect(idx[:]))
-        v_codes = [
-            [held([P, BANK], U32, "v_codes%d_%d" % (a, h), "scale_windows" if a + h == 0 else None) for h in range(HALVES)]
-            for a in range(PASSES)
-        ]
+        v_codes = [[held([P, BANK], U32, "v_codes%d_%d" % (a, h)) for h in range(HALVES)] for a in range(PASSES)]
 
         def gather_words(a):
             for h in range(HALVES):
@@ -105,38 +115,33 @@ def tile_list_calf_block_scores_kernel(
         wga_sb = placed([P, M], F32, "wga_sb", 8)
         nc.sync.dma_start(wga_sb[:], wga)
         w3_raw = [load_rows(w3, 0, placed([P, PACK, H], F32, "w3_raw0", 11))]
-        w2_plane = placed([P, PASSES * H], U8, "w2_plane", 10)
-        nc.vector.tensor_copy(
-            w2_plane[:].rearrange("p (a t m) -> p a m t", a=PASSES, t=PACK),
-            w2_scales_raw[:].bitcast(U8).rearrange("p (a m t) -> p a m t", a=PASSES, t=PACK),
-        )
 
         gather_words(1)
         w3_raw.append(load_rows(w3, 1, placed([P, PACK, H], F32, "w3_raw1", 19)))
+        w4_raw = load_rows(w4, 0, placed([P, PACK, H], F32, "w4_raw", 32))
         wgb_sb = placed([P, M], F32, "wgb_sb", 27)
         nc.sync.dma_start(wgb_sb[:], wgb)
         gain_sb = placed([P, PACK], F32, "gain_sb", 31)
         nc.sync.dma_start(gain_sb[:], gain.rearrange("(p t) -> p t", t=PACK))
-        w4_raw = load_rows(w4, 0, placed([P, PACK, H], F32, "w4_raw", 32))
         w5_codes = placed([P, N], I32, "w5_codes", 29)
         nc.sync.dma_start(w5_codes[:], w5_words[0].rearrange("p c i -> p (c i)").bitcast(I32))
         w5_plane = placed([P, N // 4], I32, "w5_plane", 31.25)
-        nc.gpsimd.memset(w5_plane[:], 0)
+        nc.vector.memset(w5_plane[:], 0)
         for q in range(4):
             nc.sync.dma_start(w5_plane[32 * q : 32 * q + 4, :], w5_scales[0, 4 * q : 4 * q + 4, :].bitcast(I32))
         b5_sb = placed([P, N // P], F32, "b5_sb", 31.125)
         with nc.allow_non_contiguous_dma(reason="one bias value a partition"):
             nc.sync.dma_start(b5_sb[:], b5.rearrange("(c p) -> p c", p=P))
 
-        def first_stage(codes_of, plane_of, fmt, t, h):
-            acc = psum.tile([P, BANK], F32, name="acc", tag="acc")
+        def first_stage(codes_of, plane_of, fmt, t, h, reader):
+            acc = psum.tile([P, BANK], F32, name="acc", tag=reader)
             for a in range(PASSES):
                 nc.tensor.matmul_mx(
                     out=acc[:],
                     lhsT=codes_of(a, t).bitcast(fmt),
                     lhsT_scale=plane_of(a, t),
                     rhs=v_codes[a][h][:].bitcast(FP8X4),
-                    rhs_scale=v_planes[a][:, BANK * h : BANK * (h + 1)],
+                    rhs_scale=planes[:].bitcast(U8)[:, (S + H) * a + BANK * h : (S + H) * a + BANK * (h + 1)],
                     start=(a == 0),
                     stop=(a == PASSES - 1),
                 )
@@ -145,8 +150,8 @@ def tile_list_calf_block_scores_kernel(
         def round_dealt(copy, raw, name):
             grouped = held([P, PACK * H], BF16, name)
             copy(
-                grouped[:].rearrange("p (t m j) -> p m j t", t=PACK, j=PACK),
-                raw[:].rearrange("p j (m t) -> p m j t", t=PACK),
+                grouped[:].rearrange("p (t m j) -> p m t j", t=PACK, j=PACK),
+                raw[:].rearrange("p j (m t) -> p m t j", t=PACK),
             )
             return grouped
 
@@ -165,38 +170,41 @@ def tile_list_calf_block_scores_kernel(
 
         w1_q = [quantize(round_dealt(nc.scalar.copy, w1_raw[0], "w1_bf0"), "w1_0", 1)]
 
+        def stage_of(q, t, h, reader):
+            return first_stage(
+                lambda a, t: q[a][0][:, P * t : P * (t + 1)], lambda a, t: q[a][1][:, P * t : P * (t + 1)], FP8X4, t, h, reader
+            )
+
         d2b = [held([P, S], F32, "d2b%d" % t) for t in range(PACK)]
-        for t in range(PACK):
+        xa = [held([P, M], F32, "xa%d" % t) for t in range(PACK)]
+
+        def second_reading(t):
             for h in range(HALVES):
                 acc = first_stage(
                     lambda a, t: w2_codes[:, H * a + P * t : H * a + P * (t + 1)],
-                    lambda a, t: w2_plane[:, H * a + P * t : H * a + P * (t + 1)],
-                    FP4X4, t, h,
+                    lambda a, t: planes[:].bitcast(U8)[:, (S + H) * a + S + P * t : (S + H) * a + S + P * (t + 1)],
+                    FP4X4, t, h, "scalar",
                 )
                 nc.scalar.activation(d2b[t][:, BANK * h : BANK * (h + 1)], acc[:], ACT.Identity, bias=b2_sb[:, t : t + 1])
 
-        w1_q.append(quantize(round_dealt(nc.vector.tensor_copy, w1_raw[1], "w1_bf1"), "w1_1", 2))
-        w3_q = [quantize(round_dealt(nc.scalar.copy, w3_raw[a], "w3_bf%d" % a), "w3_%d" % a, 1) for a in range(PASSES)]
-
-        def stage_of(q, t, h):
-            return first_stage(
-                lambda a, t: q[a][0][:, P * t : P * (t + 1)], lambda a, t: q[a][1][:, P * t : P * (t + 1)], FP8X4, t, h
-            )
-
-        xa = [held([P, M], F32, "xa%d" % t) for t in range(PACK)]
-        for t in range(PACK):
-            ha = held([P, S], F32, "ha%d" % t, after="w3_bf1" if t == PACK - 1 else None)
+        def bull_side(t, after=None):
+            ha = held([P, S], F32, "ha%d" % t, after)
             for h in range(HALVES):
-                acc = stage_of(w1_q, t, h)
+                acc = stage_of(w1_q, t, h, "vector")
                 cols = slice(BANK * h, BANK * (h + 1))
                 nc.vector.tensor_tensor(ha[:, cols], acc[:], d2b[t][:, cols], ALU.mult)
             nc.vector.tensor_tensor(xa[t][:], ha[:].indirect(idx_a[:]), wga_sb[:], ALU.mult)
 
-        hb = [held([P, S], F32, "hb%d" % t) for t in range(PACK)]
-        for t in range(PACK):
-            for h in range(HALVES):
-                acc = stage_of(w3_q, t, h)
-                nc.scalar.copy(hb[t][:, BANK * h : BANK * (h + 1)], acc[:])
+        second_reading(0)
+        second_reading(1)
+        w1_q.append(quantize(round_dealt(nc.vector.tensor_copy, w1_raw[1], "w1_bf1"), "w1_1", 4))
+        bull_side(0)
+        second_reading(2)
+        second_reading(3)
+        w3_q = [quantize(round_dealt(nc.scalar.copy, w3_raw[a], "w3_bf%d" % a), "w3_%d" % a, 1) for a in range(PASSES)]
+        bull_side(1)
+        bull_side(2)
+        bull_side(3, after="w3_bf1")
 
         w4_bf = held([P, PACK * N], BF16, "w4_bf")
         for c in range(0, N, P):
@@ -204,47 +212,66 @@ def tile_list_calf_block_scores_kernel(
                 w4_bf[:, PACK * c : PACK * (c + P)].rearrange("p (c i j) -> p c j i", i=4, j=PACK),
                 w4_raw[:, :, c : c + P].rearrange("p j (c i) -> p c j i", i=4),
             )
+
+        hb = [held([P, S], F32, "hb%d" % t) for t in range(PACK)]
+        for t in range(PACK):
+            for h in range(HALVES):
+                acc = stage_of(w3_q, t, h, "scalar")
+                nc.scalar.copy(hb[t][:, BANK * h : BANK * (h + 1)], acc[:])
+
         w4_codes, w4_plane = quantize(w4_bf, "w4", 1)
 
-        for part in range(M // M_PART):
-            cols = slice(M_PART * part, M_PART * (part + 1))
-            x_rows = held([P, PACK, M_PART], BF16, "x_rows%d" % part)
+        def bend(part, behind):
+            cols = M_PARTS[part]
+            width = cols.stop - cols.start
+            x_rows = held([P, PACK, width], BF16, "x_rows%d" % part)
             for t in range(PACK):
-                xb = work.tile([P, M_PART], F32, name="xb")
+                xb = held([P, width], F32, "xb", behind.get(t, "xb%d" % (t % 2)))
                 nc.vector.tensor_tensor(
-                    xb[:], hb[t][:].indirect(idx_b[:, M_PART // 16 * part : M_PART // 16 * (part + 1)]), wgb_sb[:, cols], ALU.mult
+                    xb[:], hb[t][:].indirect(idx_b[:, cols.start // 16 : cols.stop // 16]), wgb_sb[:, cols], ALU.mult
                 )
-                z = work.tile([P, M_PART], F32, name="z")
+                z = work.tile([P, width], F32, name="z")
                 nc.vector.tensor_tensor(z[:], xa[t][:, cols], xb[:], ALU.add)
-                bent = work.tile([P, M_PART], F32, name="bent")
+                bent = work.tile([P, width], F32, name="bent")
                 nc.scalar.activation(bent[:], z[:], ACT.Tanh)
                 nc.scalar.activation(x_rows[:, t, :], bent[:], ACT.Copy, scale=gain_sb[:, t : t + 1])
-            x_bf = held([P, PACK * M_PART], BF16, "x_bf%d" % part)
+            return x_rows
+
+        def quantize_x(part, x_rows):
+            x_bf = held([P, PACK * x_rows.shape[2]], BF16, "x_bf%d" % part)
             nc.vector.tensor_copy(
                 x_bf[:].rearrange("p (c i t) -> p c t i", i=4, t=PACK), x_rows[:].rearrange("p t (c i) -> p c t i", i=4)
             )
-            x_codes, x_plane = quantize(x_bf, "x%d" % part, 1)
+            return quantize(x_bf, "x%d" % part, 1)
+
+        def score(part, x_q):
+            x_codes, x_plane = x_q
+            cols = M_PARTS[part]
+            width = cols.stop - cols.start
             for pair in range(N // P // 2):
-                y4 = psum.tile([P, 2, M_PART], F32, name="y4", tag="acc")
-                y5 = psum.tile([P, 2, M_PART], F32, name="y5", tag="acc")
-                y5b = held([P, 2, M_PART], F32, "y5b%d_%d" % (part, pair))
-                for i in range(2):
-                    n_cols = slice(P * (2 * pair + i), P * (2 * pair + i + 1))
-                    nc.tensor.matmul_mx(
-                        out=y5[:, i, :], lhsT=w5_codes[:, n_cols].bitcast(FP8X4), lhsT_scale=w5_plane[:].bitcast(U8)[:, n_cols],
-                        rhs=x_codes[:].bitcast(FP8X4), rhs_scale=x_plane[:], start=True, stop=True,
-                    )
-                for i in range(2):
-                    n_cols = slice(P * (2 * pair + i), P * (2 * pair + i + 1))
-                    nc.tensor.matmul_mx(
-                        out=y4[:, i, :], lhsT=w4_codes[:, n_cols].bitcast(FP8X4), lhsT_scale=w4_plane[:, n_cols],
-                        rhs=x_codes[:].bitcast(FP8X4), rhs_scale=x_plane[:], start=True, stop=True,
-                    )
+                y4 = psum.tile([P, 2, width], F32, name="y4", tag="vector")
+                y5 = psum.tile([P, 2, width], F32, name="y5", tag="scalar")
+                y5b = held([P, 2, width], F32, "y5b%d_%d" % (part, pair))
+                for acc, codes, plane in ((y5, w5_codes, w5_plane[:].bitcast(U8)), (y4, w4_codes, w4_plane[:])):
+                    for i in range(2):
+                        n_cols = slice(P * (2 * pair + i), P * (2 * pair + i + 1))
+                        nc.tensor.matmul_mx(
+                            out=acc[:, i, :], lhsT=codes[:, n_cols].bitcast(FP8X4), lhsT_scale=plane[:, n_cols],
+                            rhs=x_codes[:].bitcast(FP8X4), rhs_scale=x_plane[:], start=True, stop=True,
+                        )
                 for i in range(2):
                     c = 2 * pair + i
                     nc.scalar.activation(y5b[:, i, :], y5[:, i, :], ACT.Identity, bias=b5_sb[:, c : c + 1])
-                best = held([P, 2, M_PART], F32, "best%d_%d" % (part, pair))
+                best = held([P, 2, width], F32, "best%d_%d" % (part, pair))
                 nc.vector.tensor_tensor(best[:], y4[:], y5b[:], ALU.max)
                 nc.sync.dma_start(
                     out[2 * P * pair : 2 * P * (pair + 1), cols].rearrange("(i p) m -> p i m", p=P), best[:]
                 )
+
+        x_0 = quantize_x(0, bend(0, {}))
+        x_1 = quantize_x(1, bend(1, {}))
+        rows_2 = bend(2, {0: "x_bf0", PACK - 1: "x_bf1"})
+        score(0, x_0)
+        x_2 = quantize_x(2, rows_2)
+        score(1, x_1)
+        score(2, x_2)

@@ -18,10 +18,35 @@ ACT = mybir.ActivationFunctionType
 
 P = 128
 PACK = 4
-PASSES = K // (P * PACK)
+K_PASS = P * PACK
+PASSES = K // K_PASS
+QUADRANT = 32
+QUADRANTS = P // QUADRANT
+BLOCKS = K_PASS // 32
 BANK = 512
 HALVES = S // BANK
+LIST_COLUMN = 16
+WORD = 4
+MOVES_AHEAD = 6
+ALIGN = 64
+
 M_PARTS = (slice(0, 256), slice(256, 384), slice(384, 512))
+
+ROWS_BYTES = PACK * H * 4
+WGT_BYTES = M * 4
+TAB0_AT = 0
+W1_PASS1_AT = TAB0_AT
+WGA_AT = W1_PASS1_AT + ROWS_BYTES
+W3_PASS0_AT = WGA_AT + WGT_BYTES
+TAB1_AT = W3_PASS0_AT + ROWS_BYTES
+W3_PASS1_AT = TAB1_AT
+WGB_AT = W3_PASS1_AT + ROWS_BYTES
+W5_CODES_AT = WGB_AT + WGT_BYTES
+GAIN_AT = W5_CODES_AT + N * WORD
+B5_AT = GAIN_AT + ALIGN
+W5_PLANE_AT = B5_AT + ALIGN
+W4_AT = W5_PLANE_AT + N
+assert W3_PASS0_AT < TAB0_AT + T * WORD <= TAB1_AT and W4_AT < TAB1_AT + T * WORD
 
 
 def tile_list_calf_block_scores_kernel(
@@ -31,117 +56,126 @@ def tile_list_calf_block_scores_kernel(
     with ExitStack() as ctx:
         keep = ctx.enter_context(tc.tile_pool(name="keep", bufs=1))
         stream = ctx.enter_context(tc.tile_pool(name="stream", bufs=1))
-        work = ctx.enter_context(tc.tile_pool(name="work", bufs=4))
+        work = ctx.enter_context(tc.tile_pool(name="work", bufs=PACK))
         psum = ctx.enter_context(tc.psum_pool(name="psum", bufs=4))
 
-        def held(shape, dtype, name, after=None):
-            return keep.tile(shape, dtype, name=name, tag=after or name, align_bytes=64)
+        def held(shape, dtype, name, reuses=None):
+            return keep.tile(shape, dtype, name=name, tag=reuses or name, align_bytes=ALIGN)
 
-        def placed(shape, dtype, name, kib):
-            return stream.tile(shape, dtype, name=name, align_bytes=64, offset=int(1024 * kib))
+        def placed(shape, dtype, name, at):
+            return stream.tile(shape, dtype, name=name, align_bytes=ALIGN, offset=at)
 
-        rows = PASSES * 16
-        scale_window = held([P, T // 4], I32, "scale_window")
-        w2_scales_raw = held([P, H // 4], I32, "w2_scales_raw")
-        for tile in (scale_window, w2_scales_raw):
-            nc.vector.memset(tile[rows:64, :], 0)
-            nc.vector.memset(tile[64:P, :], 0)
-        planes = held([P, PASSES * (S + H) // 4], I32, "planes")
+        scale_row_count = PASSES * BLOCKS
+        scale_window = held([P, T // WORD], I32, "scale_window")
+        w2_scales_raw = held([P, H // WORD], I32, "w2_scales_raw")
+        for rows_tile in (scale_window, w2_scales_raw):
+            nc.vector.memset(rows_tile[scale_row_count : P // 2, :], 0)
+            nc.vector.memset(rows_tile[P // 2 : P, :], 0)
+        plane_width = S + H
+        planes = held([P, PASSES * plane_width // WORD], I32, "planes")
         nc.vector.memset(planes[:], 0)
 
-        idx = keep.tile([P, S // 16], U16, name="idx")
+        idx = keep.tile([P, S // LIST_COLUMN], U16, name="idx")
         nc.sync.dma_start(idx[:], offs)
-        nc.sync.dma_start(scale_window[0:rows, :], tab_scales.rearrange("a q t -> (a q) t").bitcast(I32))
-        nc.sync.dma_start(w2_scales_raw[0:rows, :], w2_scales.rearrange("a q c -> (a q) c").bitcast(I32))
-        w2_raw = held([P, PASSES * H // 2], I32, "w2_raw")
+        nc.sync.dma_start(scale_window[0:scale_row_count, :], tab_scales.rearrange("a q t -> (a q) t").bitcast(I32))
+        nc.sync.dma_start(w2_scales_raw[0:scale_row_count, :], w2_scales.rearrange("a q c -> (a q) c").bitcast(I32))
+        w2_raw = held([P, PASSES * H * 2 // WORD], I32, "w2_raw")
         nc.sync.dma_start(
             w2_raw[:].rearrange("p (a c) -> p a c", a=PASSES), w2_words.rearrange("a p c -> p a c").bitcast(I32)
         )
-        idx_a = keep.tile([P, M // 16], U16, name="idx_a")
+        idx_a = keep.tile([P, M // LIST_COLUMN], U16, name="idx_a")
         nc.sync.dma_start(idx_a[:], offs2)
-        idx_b = keep.tile([P, M // 16], U16, name="idx_b")
+        idx_b = keep.tile([P, M // LIST_COLUMN], U16, name="idx_b")
         nc.sync.dma_start(idx_b[:], offs3)
         b2_sb = held([P, PACK], F32, "b2_sb")
         nc.sync.dma_start(b2_sb[:], b2.rearrange("(p t) -> p t", t=PACK))
 
-        def load_table(a, kib):
-            words = placed([P, T], I32, "tab%d" % a, kib)
+        def load_table(a, at):
+            words = placed([P, T], I32, "tab%d" % a, at)
             nc.sync.dma_start(words[:], tab_words[a].rearrange("p t i -> p (t i)").bitcast(I32))
             return words
 
         def load_rows(w, a, raw):
-            nc.sync.dma_start(raw[:], w[512 * a : 512 * (a + 1), :].rearrange("(p j) c -> p j c", j=PACK))
+            nc.sync.dma_start(raw[:], w[K_PASS * a : K_PASS * (a + 1), :].rearrange("(p j) c -> p j c", j=PACK))
             return raw
 
-        tab = [load_table(0, 0)]
-        w1_raw = [load_rows(w1, 0, placed([P, PACK, H], F32, "w1_raw0", 35))]
+        tab = [load_table(0, TAB0_AT), load_table(1, TAB1_AT)]
 
-        picked_scales = placed([P, S], U8, "picked_scales", 19)
+        picked_scales = held([P, S], U8, "picked_scales")
         nc.vector.tensor_copy(picked_scales[:], scale_window[:].bitcast(U8).indirect(idx[:]))
-        scale_rows = held([P, S + H], U8, "scale_rows")
+        scale_rows = held([P, plane_width], U8, "scale_rows")
         nc.vector.tensor_copy(
-            scale_rows[:, S:].rearrange("p (t m) -> p m t", t=PACK),
-            w2_scales_raw[:].bitcast(U8).rearrange("p (m t) -> p m t", t=PACK),
+            scale_rows[:, S:].rearrange("p (t c) -> p t c", t=PACK),
+            w2_scales_raw[:].bitcast(U8).rearrange("p (c t) -> p t c", t=PACK),
         )
         nc.vector.tensor_copy(scale_rows[:, :S].bitcast(I32), picked_scales[:].bitcast(I32))
 
         def place_scale_rows(a, q):
-            width = (S + H) // 4
-            first = 16 * a + 4 * q
+            words = plane_width // WORD
+            first = BLOCKS * a + 4 * q
             nc.sync.dma_start(
-                planes[32 * q : 32 * q + 4, width * a : width * (a + 1)], scale_rows[first : first + 4, :].bitcast(I32)
+                planes[QUADRANT * q : QUADRANT * q + 4, words * a : words * (a + 1)],
+                scale_rows[first : first + 4, :].bitcast(I32),
             )
 
-        for q in range(4):
-            place_scale_rows(0, q)
-        tab.append(load_table(1, 19))
-        for q in range(4):
-            place_scale_rows(1, q)
+        moves = [(a, q) for a in range(PASSES) for q in range(QUADRANTS)]
+        for a, q in moves[:MOVES_AHEAD]:
+            place_scale_rows(a, q)
+        w1_raw = [load_rows(w1, 0, held([P, PACK, H], F32, "w1_raw0", reuses="picked_scales"))]
+        for a, q in moves[MOVES_AHEAD:]:
+            place_scale_rows(a, q)
 
         w2_codes = held([P, PASSES * H], U16, "w2_codes")
         nc.vector.tensor_copy(
-            w2_codes[:].rearrange("p (a t m) -> p a m t", a=PASSES, t=PACK),
-            w2_raw[:].bitcast(U16).rearrange("p (a m t) -> p a m t", a=PASSES, t=PACK),
+            w2_codes[:].rearrange("p (a t c) -> p a t c", a=PASSES, t=PACK),
+            w2_raw[:].bitcast(U16).rearrange("p (a c t) -> p a t c", a=PASSES, t=PACK),
         )
 
         v_codes = [[held([P, BANK], U32, "v_codes%d_%d" % (a, h)) for h in range(HALVES)] for a in range(PASSES)]
 
         def gather_words(a):
+            columns = BANK // LIST_COLUMN
             for h in range(HALVES):
-                nc.vector.tensor_copy(v_codes[a][h][:], tab[a][:].bitcast(U32).indirect(idx[:, 32 * h : 32 * (h + 1)]))
+                nc.vector.tensor_copy(
+                    v_codes[a][h][:], tab[a][:].bitcast(U32).indirect(idx[:, columns * h : columns * (h + 1)])
+                )
 
         gather_words(0)
-        w1_raw.append(load_rows(w1, 1, placed([P, PACK, H], F32, "w1_raw1", 0)))
-        wga_sb = placed([P, M], F32, "wga_sb", 8)
+        w1_raw.append(load_rows(w1, 1, placed([P, PACK, H], F32, "w1_raw1", W1_PASS1_AT)))
+        wga_sb = placed([P, M], F32, "wga_sb", WGA_AT)
         nc.sync.dma_start(wga_sb[:], wga)
-        w3_raw = [load_rows(w3, 0, placed([P, PACK, H], F32, "w3_raw0", 11))]
+        w3_raw = [load_rows(w3, 0, placed([P, PACK, H], F32, "w3_raw0", W3_PASS0_AT))]
 
         gather_words(1)
-        w3_raw.append(load_rows(w3, 1, placed([P, PACK, H], F32, "w3_raw1", 19)))
-        w4_raw = load_rows(w4, 0, placed([P, PACK, H], F32, "w4_raw", 32))
-        wgb_sb = placed([P, M], F32, "wgb_sb", 27)
+        w3_raw.append(load_rows(w3, 1, placed([P, PACK, H], F32, "w3_raw1", W3_PASS1_AT)))
+        w4_raw = load_rows(w4, 0, placed([P, PACK, N], F32, "w4_raw", W4_AT))
+        wgb_sb = placed([P, M], F32, "wgb_sb", WGB_AT)
         nc.sync.dma_start(wgb_sb[:], wgb)
-        gain_sb = placed([P, PACK], F32, "gain_sb", 31)
+        gain_sb = placed([P, PACK], F32, "gain_sb", GAIN_AT)
         nc.sync.dma_start(gain_sb[:], gain.rearrange("(p t) -> p t", t=PACK))
-        w5_codes = placed([P, N], I32, "w5_codes", 29)
+        w5_codes = placed([P, N], I32, "w5_codes", W5_CODES_AT)
         nc.sync.dma_start(w5_codes[:], w5_words[0].rearrange("p c i -> p (c i)").bitcast(I32))
-        w5_plane = placed([P, N // 4], I32, "w5_plane", 31.25)
-        nc.vector.memset(w5_plane[:], 0)
-        for q in range(4):
-            nc.sync.dma_start(w5_plane[32 * q : 32 * q + 4, :], w5_scales[0, 4 * q : 4 * q + 4, :].bitcast(I32))
-        b5_sb = placed([P, N // P], F32, "b5_sb", 31.125)
-        with nc.allow_non_contiguous_dma(reason="one bias value a partition"):
+        w5_plane = placed([P, N // WORD], I32, "w5_plane", W5_PLANE_AT)
+        nc.gpsimd.memset(w5_plane[:], 0)
+        for q in range(QUADRANTS):
+            nc.sync.dma_start(
+                w5_plane[QUADRANT * q : QUADRANT * q + 4, :], w5_scales[0, 4 * q : 4 * q + 4, :].bitcast(I32)
+            )
+        b5_sb = placed([P, N // P], F32, "b5_sb", B5_AT)
+        with nc.allow_non_contiguous_dma(reason="output row 128 c + p takes its bias on partition p"):
             nc.sync.dma_start(b5_sb[:], b5.rearrange("(c p) -> p c", p=P))
 
-        def first_stage(codes_of, plane_of, fmt, t, h, reader):
+        def first_stage(weights, fmt, t, h, reader):
             acc = psum.tile([P, BANK], F32, name="acc", tag=reader)
+            channels = slice(P * t, P * (t + 1))
             for a in range(PASSES):
+                codes, plane = weights[a]
                 nc.tensor.matmul_mx(
                     out=acc[:],
-                    lhsT=codes_of(a, t).bitcast(fmt),
-                    lhsT_scale=plane_of(a, t),
+                    lhsT=codes[:, channels].bitcast(fmt),
+                    lhsT_scale=plane[:, channels],
                     rhs=v_codes[a][h][:].bitcast(FP8X4),
-                    rhs_scale=planes[:].bitcast(U8)[:, (S + H) * a + BANK * h : (S + H) * a + BANK * (h + 1)],
+                    rhs_scale=planes[:].bitcast(U8)[:, plane_width * a + BANK * h : plane_width * a + BANK * (h + 1)],
                     start=(a == 0),
                     stop=(a == PASSES - 1),
                 )
@@ -150,12 +184,12 @@ def tile_list_calf_block_scores_kernel(
         def round_dealt(copy, raw, name):
             grouped = held([P, PACK * H], BF16, name)
             copy(
-                grouped[:].rearrange("p (t m j) -> p m t j", t=PACK, j=PACK),
-                raw[:].rearrange("p j (m t) -> p m t j", t=PACK),
+                grouped[:].rearrange("p (t c j) -> p c t j", t=PACK, j=PACK),
+                raw[:].rearrange("p j (c t) -> p c t j", t=PACK),
             )
             return grouped
 
-        def quantize(grouped, name, pieces):
+        def quantize(grouped, name, pieces=1):
             width = grouped.shape[1] // PACK
             codes = held([P, width], U32, name + "_codes")
             plane = held([P, width], U8, name + "_plane")
@@ -166,70 +200,65 @@ def tile_list_calf_block_scores_kernel(
                     scales=plane[:, c : c + step],
                     in_=grouped[:, PACK * c : PACK * (c + step)],
                 )
-            return codes, plane
+            return codes[:], plane[:]
 
-        w1_q = [quantize(round_dealt(nc.scalar.copy, w1_raw[0], "w1_bf0"), "w1_0", 1)]
-
-        def stage_of(q, t, h, reader):
-            return first_stage(
-                lambda a, t: q[a][0][:, P * t : P * (t + 1)], lambda a, t: q[a][1][:, P * t : P * (t + 1)], FP8X4, t, h, reader
-            )
+        w1_q = [quantize(round_dealt(nc.vector.tensor_copy, w1_raw[0], "w1_bf0"), "w1_0")]
+        w2_q = [
+            (w2_codes[:, H * a : H * (a + 1)], planes[:].bitcast(U8)[:, plane_width * a + S : plane_width * (a + 1)])
+            for a in range(PASSES)
+        ]
 
         d2b = [held([P, S], F32, "d2b%d" % t) for t in range(PACK)]
         xa = [held([P, M], F32, "xa%d" % t) for t in range(PACK)]
 
         def second_reading(t):
             for h in range(HALVES):
-                acc = first_stage(
-                    lambda a, t: w2_codes[:, H * a + P * t : H * a + P * (t + 1)],
-                    lambda a, t: planes[:].bitcast(U8)[:, (S + H) * a + S + P * t : (S + H) * a + S + P * (t + 1)],
-                    FP4X4, t, h, "scalar",
-                )
+                acc = first_stage(w2_q, FP4X4, t, h, "scalar")
                 nc.scalar.activation(d2b[t][:, BANK * h : BANK * (h + 1)], acc[:], ACT.Identity, bias=b2_sb[:, t : t + 1])
 
-        def bull_side(t, after=None):
-            ha = held([P, S], F32, "ha%d" % t, after)
+        def bull_side(t, reuses=None):
+            ha = held([P, S], F32, "ha%d" % t, reuses)
             for h in range(HALVES):
-                acc = stage_of(w1_q, t, h, "vector")
+                acc = first_stage(w1_q, FP8X4, t, h, "vector")
                 cols = slice(BANK * h, BANK * (h + 1))
                 nc.vector.tensor_tensor(ha[:, cols], acc[:], d2b[t][:, cols], ALU.mult)
             nc.vector.tensor_tensor(xa[t][:], ha[:].indirect(idx_a[:]), wga_sb[:], ALU.mult)
 
         second_reading(0)
         second_reading(1)
-        w1_q.append(quantize(round_dealt(nc.vector.tensor_copy, w1_raw[1], "w1_bf1"), "w1_1", 4))
+        w1_q.append(quantize(round_dealt(nc.vector.tensor_copy, w1_raw[1], "w1_bf1"), "w1_1", pieces=PACK))
         bull_side(0)
         second_reading(2)
         second_reading(3)
-        w3_q = [quantize(round_dealt(nc.scalar.copy, w3_raw[a], "w3_bf%d" % a), "w3_%d" % a, 1) for a in range(PASSES)]
+        w3_q = [quantize(round_dealt(nc.scalar.copy, w3_raw[a], "w3_bf%d" % a), "w3_%d" % a) for a in range(PASSES)]
         bull_side(1)
         bull_side(2)
-        bull_side(3, after="w3_bf1")
+        bull_side(3, reuses="w3_bf1")
 
         w4_bf = held([P, PACK * N], BF16, "w4_bf")
         for c in range(0, N, P):
             nc.scalar.copy(
-                w4_bf[:, PACK * c : PACK * (c + P)].rearrange("p (c i j) -> p c j i", i=4, j=PACK),
-                w4_raw[:, :, c : c + P].rearrange("p j (c i) -> p c j i", i=4),
+                w4_bf[:, PACK * c : PACK * (c + P)].rearrange("p (c j) -> p c j", j=PACK),
+                w4_raw[:, :, c : c + P].rearrange("p j c -> p c j"),
             )
 
         hb = [held([P, S], F32, "hb%d" % t) for t in range(PACK)]
         for t in range(PACK):
             for h in range(HALVES):
-                acc = stage_of(w3_q, t, h, "scalar")
+                acc = first_stage(w3_q, FP8X4, t, h, "scalar")
                 nc.scalar.copy(hb[t][:, BANK * h : BANK * (h + 1)], acc[:])
 
-        w4_codes, w4_plane = quantize(w4_bf, "w4", 1)
+        w4_q = quantize(w4_bf, "w4")
+        w5_q = (w5_codes[:], w5_plane[:].bitcast(U8))
 
-        def bend(part, behind):
+        def bend(part, reuses):
             cols = M_PARTS[part]
             width = cols.stop - cols.start
             x_rows = held([P, PACK, width], BF16, "x_rows%d" % part)
             for t in range(PACK):
-                xb = held([P, width], F32, "xb", behind.get(t, "xb%d" % (t % 2)))
-                nc.vector.tensor_tensor(
-                    xb[:], hb[t][:].indirect(idx_b[:, cols.start // 16 : cols.stop // 16]), wgb_sb[:, cols], ALU.mult
-                )
+                xb = held([P, width], F32, "xb", reuses.get(t, "xb%d" % (t % 2)))
+                picks = idx_b[:, cols.start // LIST_COLUMN : cols.stop // LIST_COLUMN]
+                nc.vector.tensor_tensor(xb[:], hb[t][:].indirect(picks), wgb_sb[:, cols], ALU.mult)
                 z = work.tile([P, width], F32, name="z")
                 nc.vector.tensor_tensor(z[:], xa[t][:, cols], xb[:], ALU.add)
                 bent = work.tile([P, width], F32, name="bent")
@@ -239,29 +268,32 @@ def tile_list_calf_block_scores_kernel(
 
         def quantize_x(part, x_rows):
             x_bf = held([P, PACK * x_rows.shape[2]], BF16, "x_bf%d" % part)
-            nc.vector.tensor_copy(
-                x_bf[:].rearrange("p (c i t) -> p c t i", i=4, t=PACK), x_rows[:].rearrange("p t (c i) -> p c t i", i=4)
-            )
-            return quantize(x_bf, "x%d" % part, 1)
+            nc.vector.tensor_copy(x_bf[:].rearrange("p (m t) -> p m t", t=PACK), x_rows[:].rearrange("p t m -> p m t"))
+            return quantize(x_bf, "x%d" % part)
 
         def score(part, x_q):
             x_codes, x_plane = x_q
             cols = M_PARTS[part]
             width = cols.stop - cols.start
-            for pair in range(N // P // 2):
+            for pair in range(N // (2 * P)):
                 y4 = psum.tile([P, 2, width], F32, name="y4", tag="vector")
                 y5 = psum.tile([P, 2, width], F32, name="y5", tag="scalar")
                 y5b = held([P, 2, width], F32, "y5b%d_%d" % (part, pair))
-                for acc, codes, plane in ((y5, w5_codes, w5_plane[:].bitcast(U8)), (y4, w4_codes, w4_plane[:])):
+                for acc, (codes, plane) in ((y5, w5_q), (y4, w4_q)):
                     for i in range(2):
                         n_cols = slice(P * (2 * pair + i), P * (2 * pair + i + 1))
                         nc.tensor.matmul_mx(
-                            out=acc[:, i, :], lhsT=codes[:, n_cols].bitcast(FP8X4), lhsT_scale=plane[:, n_cols],
-                            rhs=x_codes[:].bitcast(FP8X4), rhs_scale=x_plane[:], start=True, stop=True,
+                            out=acc[:, i, :],
+                            lhsT=codes[:, n_cols].bitcast(FP8X4),
+                            lhsT_scale=plane[:, n_cols],
+                            rhs=x_codes.bitcast(FP8X4),
+                            rhs_scale=x_plane,
+                            start=True,
+                            stop=True,
                         )
                 for i in range(2):
-                    c = 2 * pair + i
-                    nc.scalar.activation(y5b[:, i, :], y5[:, i, :], ACT.Identity, bias=b5_sb[:, c : c + 1])
+                    n_tile = 2 * pair + i
+                    nc.scalar.activation(y5b[:, i, :], y5[:, i, :], ACT.Identity, bias=b5_sb[:, n_tile : n_tile + 1])
                 best = held([P, 2, width], F32, "best%d_%d" % (part, pair))
                 nc.vector.tensor_tensor(best[:], y4[:], y5b[:], ALU.max)
                 nc.sync.dma_start(

from contextlib import ExitStack

import concourse.mybir as mybir

K, H, N, T, S, M = 1024, 512, 512, 4096, 1024, 512
FLOPS = 2 * (3 * K * H * S + 2 * H * N * M)

F32 = mybir.dt.float32
BF16 = mybir.dt.bfloat16
I32 = mybir.dt.int32
U32 = mybir.dt.uint32
U16 = mybir.dt.uint16
U8 = mybir.dt.uint8
FP8X4 = mybir.dt.float8_e4m3fn_x4
FP4X4 = mybir.dt.float4_e2m1fn_x4
ALU = mybir.AluOpType
ACT = mybir.ActivationFunctionType

P = 128
PACK = 4
K_PASS = P * PACK
PASSES = K // K_PASS
QUADRANT = 32
QUADRANTS = P // QUADRANT
BLOCKS = K_PASS // 32
BANK = 512
HALVES = S // BANK
LIST_COLUMN = 16
WORD = 4
MOVES_AHEAD = 6
ALIGN = 64

M_PARTS = (slice(0, 256), slice(256, 384), slice(384, 512))

ROWS_BYTES = PACK * H * 4
WGT_BYTES = M * 4
TAB0_AT = 0
W1_PASS1_AT = TAB0_AT
WGA_AT = W1_PASS1_AT + ROWS_BYTES
W3_PASS0_AT = WGA_AT + WGT_BYTES
TAB1_AT = W3_PASS0_AT + ROWS_BYTES
W3_PASS1_AT = TAB1_AT
WGB_AT = W3_PASS1_AT + ROWS_BYTES
W5_CODES_AT = WGB_AT + WGT_BYTES
GAIN_AT = W5_CODES_AT + N * WORD
B5_AT = GAIN_AT + ALIGN
W5_PLANE_AT = B5_AT + ALIGN
W4_AT = W5_PLANE_AT + N
assert W3_PASS0_AT < TAB0_AT + T * WORD <= TAB1_AT and W4_AT < TAB1_AT + T * WORD


def tile_list_calf_block_scores_kernel(
    tc, tab_words, tab_scales, offs, offs2, offs3, w1, w2_words, w2_scales, b2, w3, wga, wgb, gain, w4, w5_words, w5_scales, b5, out
):
    nc = tc.nc
    with ExitStack() as ctx:
        keep = ctx.enter_context(tc.tile_pool(name="keep", bufs=1))
        stream = ctx.enter_context(tc.tile_pool(name="stream", bufs=1))
        work = ctx.enter_context(tc.tile_pool(name="work", bufs=PACK))
        psum = ctx.enter_context(tc.psum_pool(name="psum", bufs=4))

        def held(shape, dtype, name, reuses=None):
            return keep.tile(shape, dtype, name=name, tag=reuses or name, align_bytes=ALIGN)

        def placed(shape, dtype, name, at):
            return stream.tile(shape, dtype, name=name, align_bytes=ALIGN, offset=at)

        scale_row_count = PASSES * BLOCKS
        scale_window = held([P, T // WORD], I32, "scale_window")
        w2_scales_raw = held([P, H // WORD], I32, "w2_scales_raw")
        for rows_tile in (scale_window, w2_scales_raw):
            nc.vector.memset(rows_tile[scale_row_count : P // 2, :], 0)
            nc.vector.memset(rows_tile[P // 2 : P, :], 0)
        plane_width = S + H
        planes = held([P, PASSES * plane_width // WORD], I32, "planes")
        nc.vector.memset(planes[:], 0)

        idx = keep.tile([P, S // LIST_COLUMN], U16, name="idx")
        nc.sync.dma_start(idx[:], offs)
        nc.sync.dma_start(scale_window[0:scale_row_count, :], tab_scales.rearrange("a q t -> (a q) t").bitcast(I32))
        nc.sync.dma_start(w2_scales_raw[0:scale_row_count, :], w2_scales.rearrange("a q c -> (a q) c").bitcast(I32))
        w2_raw = held([P, PASSES * H * 2 // WORD], I32, "w2_raw")
        nc.sync.dma_start(
            w2_raw[:].rearrange("p (a c) -> p a c", a=PASSES), w2_words.rearrange("a p c -> p a c").bitcast(I32)
        )
        idx_a = keep.tile([P, M // LIST_COLUMN], U16, name="idx_a")
        nc.sync.dma_start(idx_a[:], offs2)
        idx_b = keep.tile([P, M // LIST_COLUMN], U16, name="idx_b")
        nc.sync.dma_start(idx_b[:], offs3)
        b2_sb = held([P, PACK], F32, "b2_sb")
        nc.sync.dma_start(b2_sb[:], b2.rearrange("(p t) -> p t", t=PACK))

        def load_table(a, at):
            words = placed([P, T], I32, "tab%d" % a, at)
            nc.sync.dma_start(words[:], tab_words[a].rearrange("p t i -> p (t i)").bitcast(I32))
            return words

        def load_rows(w, a, raw):
            nc.sync.dma_start(raw[:], w[K_PASS * a : K_PASS * (a + 1), :].rearrange("(p j) c -> p j c", j=PACK))
            return raw

        tab = [load_table(0, TAB0_AT), load_table(1, TAB1_AT)]

        picked_scales = held([P, S], U8, "picked_scales")
        nc.vector.tensor_copy(picked_scales[:], scale_window[:].bitcast(U8).indirect(idx[:]))
        scale_rows = held([P, plane_width], U8, "scale_rows")
        nc.vector.tensor_copy(
            scale_rows[:, S:].rearrange("p (t c) -> p t c", t=PACK),
            w2_scales_raw[:].bitcast(U8).rearrange("p (c t) -> p t c", t=PACK),
        )
        nc.vector.tensor_copy(scale_rows[:, :S].bitcast(I32), picked_scales[:].bitcast(I32))

        def place_scale_rows(a, q):
            words = plane_width // WORD
            first = BLOCKS * a + 4 * q
            nc.sync.dma_start(
                planes[QUADRANT * q : QUADRANT * q + 4, words * a : words * (a + 1)],
                scale_rows[first : first + 4, :].bitcast(I32),
            )

        moves = [(a, q) for a in range(PASSES) for q in range(QUADRANTS)]
        for a, q in moves[:MOVES_AHEAD]:
            place_scale_rows(a, q)
        w1_raw = [load_rows(w1, 0, held([P, PACK, H], F32, "w1_raw0", reuses="picked_scales"))]
        for a, q in moves[MOVES_AHEAD:]:
            place_scale_rows(a, q)

        w2_codes = held([P, PASSES * H], U16, "w2_codes")
        nc.vector.tensor_copy(
            w2_codes[:].rearrange("p (a t c) -> p a t c", a=PASSES, t=PACK),
            w2_raw[:].bitcast(U16).rearrange("p (a c t) -> p a t c", a=PASSES, t=PACK),
        )

        v_codes = [[held([P, BANK], U32, "v_codes%d_%d" % (a, h)) for h in range(HALVES)] for a in range(PASSES)]

        def gather_words(a):
            columns = BANK // LIST_COLUMN
            for h in range(HALVES):
                nc.vector.tensor_copy(
                    v_codes[a][h][:], tab[a][:].bitcast(U32).indirect(idx[:, columns * h : columns * (h + 1)])
                )

        gather_words(0)
        w1_raw.append(load_rows(w1, 1, placed([P, PACK, H], F32, "w1_raw1", W1_PASS1_AT)))
        wga_sb = placed([P, M], F32, "wga_sb", WGA_AT)
        nc.sync.dma_start(wga_sb[:], wga)
        w3_raw = [load_rows(w3, 0, placed([P, PACK, H], F32, "w3_raw0", W3_PASS0_AT))]

        gather_words(1)
        w3_raw.append(load_rows(w3, 1, placed([P, PACK, H], F32, "w3_raw1", W3_PASS1_AT)))
        w4_raw = load_rows(w4, 0, placed([P, PACK, N], F32, "w4_raw", W4_AT))
        wgb_sb = placed([P, M], F32, "wgb_sb", WGB_AT)
        nc.sync.dma_start(wgb_sb[:], wgb)
        gain_sb = placed([P, PACK], F32, "gain_sb", GAIN_AT)
        nc.sync.dma_start(gain_sb[:], gain.rearrange("(p t) -> p t", t=PACK))
        w5_codes = placed([P, N], I32, "w5_codes", W5_CODES_AT)
        nc.sync.dma_start(w5_codes[:], w5_words[0].rearrange("p c i -> p (c i)").bitcast(I32))
        w5_plane = placed([P, N // WORD], I32, "w5_plane", W5_PLANE_AT)
        nc.gpsimd.memset(w5_plane[:], 0)
        for q in range(QUADRANTS):
            nc.sync.dma_start(
                w5_plane[QUADRANT * q : QUADRANT * q + 4, :], w5_scales[0, 4 * q : 4 * q + 4, :].bitcast(I32)
            )
        b5_sb = placed([P, N // P], F32, "b5_sb", B5_AT)
        with nc.allow_non_contiguous_dma(reason="output row 128 c + p takes its bias on partition p"):
            nc.sync.dma_start(b5_sb[:], b5.rearrange("(c p) -> p c", p=P))

        def first_stage(weights, fmt, t, h, reader):
            acc = psum.tile([P, BANK], F32, name="acc", tag=reader)
            channels = slice(P * t, P * (t + 1))
            for a in range(PASSES):
                codes, plane = weights[a]
                nc.tensor.matmul_mx(
                    out=acc[:],
                    lhsT=codes[:, channels].bitcast(fmt),
                    lhsT_scale=plane[:, channels],
                    rhs=v_codes[a][h][:].bitcast(FP8X4),
                    rhs_scale=planes[:].bitcast(U8)[:, plane_width * a + BANK * h : plane_width * a + BANK * (h + 1)],
                    start=(a == 0),
                    stop=(a == PASSES - 1),
                )
            return acc

        def round_dealt(copy, raw, name):
            grouped = held([P, PACK * H], BF16, name)
            copy(
                grouped[:].rearrange("p (t c j) -> p c t j", t=PACK, j=PACK),
                raw[:].rearrange("p j (c t) -> p c t j", t=PACK),
            )
            return grouped

        def quantize(grouped, name, pieces=1):
            width = grouped.shape[1] // PACK
            codes = held([P, width], U32, name + "_codes")
            plane = held([P, width], U8, name + "_plane")
            step = width // pieces
            for c in range(0, width, step):
                nc.vector.quantize_mx(
                    out=codes[:, c : c + step].bitcast(FP8X4),
                    scales=plane[:, c : c + step],
                    in_=grouped[:, PACK * c : PACK * (c + step)],
                )
            return codes[:], plane[:]

        w1_q = [quantize(round_dealt(nc.vector.tensor_copy, w1_raw[0], "w1_bf0"), "w1_0")]
        w2_q = [
            (w2_codes[:, H * a : H * (a + 1)], planes[:].bitcast(U8)[:, plane_width * a + S : plane_width * (a + 1)])
            for a in range(PASSES)
        ]

        d2b = [held([P, S], F32, "d2b%d" % t) for t in range(PACK)]
        xa = [held([P, M], F32, "xa%d" % t) for t in range(PACK)]

        def second_reading(t):
            for h in range(HALVES):
                acc = first_stage(w2_q, FP4X4, t, h, "scalar")
                nc.scalar.activation(d2b[t][:, BANK * h : BANK * (h + 1)], acc[:], ACT.Identity, bias=b2_sb[:, t : t + 1])

        def bull_side(t, reuses=None):
            ha = held([P, S], F32, "ha%d" % t, reuses)
            for h in range(HALVES):
                acc = first_stage(w1_q, FP8X4, t, h, "vector")
                cols = slice(BANK * h, BANK * (h + 1))
                nc.vector.tensor_tensor(ha[:, cols], acc[:], d2b[t][:, cols], ALU.mult)
            nc.vector.tensor_tensor(xa[t][:], ha[:].indirect(idx_a[:]), wga_sb[:], ALU.mult)

        second_reading(0)
        second_reading(1)
        w1_q.append(quantize(round_dealt(nc.vector.tensor_copy, w1_raw[1], "w1_bf1"), "w1_1", pieces=PACK))
        bull_side(0)
        second_reading(2)
        second_reading(3)
        w3_q = [quantize(round_dealt(nc.scalar.copy, w3_raw[a], "w3_bf%d" % a), "w3_%d" % a) for a in range(PASSES)]
        bull_side(1)
        bull_side(2)
        bull_side(3, reuses="w3_bf1")

        w4_bf = held([P, PACK * N], BF16, "w4_bf")
        for c in range(0, N, P):
            nc.scalar.copy(
                w4_bf[:, PACK * c : PACK * (c + P)].rearrange("p (c j) -> p c j", j=PACK),
                w4_raw[:, :, c : c + P].rearrange("p j c -> p c j"),
            )

        hb = [held([P, S], F32, "hb%d" % t) for t in range(PACK)]
        for t in range(PACK):
            for h in range(HALVES):
                acc = first_stage(w3_q, FP8X4, t, h, "scalar")
                nc.scalar.copy(hb[t][:, BANK * h : BANK * (h + 1)], acc[:])

        w4_q = quantize(w4_bf, "w4")
        w5_q = (w5_codes[:], w5_plane[:].bitcast(U8))

        def bend(part, reuses):
            cols = M_PARTS[part]
            width = cols.stop - cols.start
            x_rows = held([P, PACK, width], BF16, "x_rows%d" % part)
            for t in range(PACK):
                xb = held([P, width], F32, "xb", reuses.get(t, "xb%d" % (t % 2)))
                picks = idx_b[:, cols.start // LIST_COLUMN : cols.stop // LIST_COLUMN]
                nc.vector.tensor_tensor(xb[:], hb[t][:].indirect(picks), wgb_sb[:, cols], ALU.mult)
                z = work.tile([P, width], F32, name="z")
                nc.vector.tensor_tensor(z[:], xa[t][:, cols], xb[:], ALU.add)
                bent = work.tile([P, width], F32, name="bent")
                nc.scalar.activation(bent[:], z[:], ACT.Tanh)
                nc.scalar.activation(x_rows[:, t, :], bent[:], ACT.Copy, scale=gain_sb[:, t : t + 1])
            return x_rows

        def quantize_x(part, x_rows):
            x_bf = held([P, PACK * x_rows.shape[2]], BF16, "x_bf%d" % part)
            nc.vector.tensor_copy(x_bf[:].rearrange("p (m t) -> p m t", t=PACK), x_rows[:].rearrange("p t m -> p m t"))
            return quantize(x_bf, "x%d" % part)

        def score(part, x_q):
            x_codes, x_plane = x_q
            cols = M_PARTS[part]
            width = cols.stop - cols.start
            for pair in range(N // (2 * P)):
                y4 = psum.tile([P, 2, width], F32, name="y4", tag="vector")
                y5 = psum.tile([P, 2, width], F32, name="y5", tag="scalar")
                y5b = held([P, 2, width], F32, "y5b%d_%d" % (part, pair))
                for acc, (codes, plane) in ((y5, w5_q), (y4, w4_q)):
                    for i in range(2):
                        n_cols = slice(P * (2 * pair + i), P * (2 * pair + i + 1))
                        nc.tensor.matmul_mx(
                            out=acc[:, i, :],
                            lhsT=codes[:, n_cols].bitcast(FP8X4),
                            lhsT_scale=plane[:, n_cols],
                            rhs=x_codes.bitcast(FP8X4),
                            rhs_scale=x_plane,
                            start=True,
                            stop=True,
                        )
                for i in range(2):
                    n_tile = 2 * pair + i
                    nc.scalar.activation(y5b[:, i, :], y5[:, i, :], ACT.Identity, bias=b5_sb[:, n_tile : n_tile + 1])
                best = held([P, 2, width], F32, "best%d_%d" % (part, pair))
                nc.vector.tensor_tensor(best[:], y4[:], y5b[:], ALU.max)
                nc.sync.dma_start(
                    out[2 * P * pair : 2 * P * (pair + 1), cols].rearrange("(i p) m -> p i m", p=P), best[:]
                )

        x_0 = quantize_x(0, bend(0, {}))
        x_1 = quantize_x(1, bend(1, {}))
        rows_2 = bend(2, {0: "x_bf0", PACK - 1: "x_bf1"})
        score(0, x_0)
        x_2 = quantize_x(2, rows_2)
        score(1, x_1)
        score(2, x_2)
